import numpy as np
import ml_dtypes


def mxq(x, axis, fmt="e4m3"):
    dtype, down = {"e4m3": (ml_dtypes.float8_e4m3fn, 7), "e5m2": (ml_dtypes.float8_e5m2, 14)}[fmt]
    v = np.moveaxis(np.asarray(x, np.float32).astype(ml_dtypes.bfloat16).astype(np.float64), axis, -1)
    blocks = v.reshape(v.shape[:-1] + (-1, 32))
    amax = np.abs(blocks).max(-1, keepdims=True)
    byte = np.maximum(np.where(amax > 0, np.frexp(amax)[1] - 1 + 127, 0) - down, 1)
    scale = np.exp2(byte - 127.0)
    codes = (blocks / scale).astype(np.float32).astype(dtype).astype(np.float64)
    return np.moveaxis((codes * scale).reshape(v.shape), -1, axis)


WIDE = False


def mx_kscale(k):
    if not WIDE:
        return np.ones(k)
    levels = np.array([10, -10, 5, -5, 0])
    if k % 512:
        return np.exp2(np.random.permutation(np.resize(levels, k // 32))).repeat(32)
    a = np.empty((k // 512, 16))
    for p in range(k // 512):
        a[p, :8] = np.random.permutation(np.resize(levels, 8))
        for g in range(8):
            far = levels[np.abs(levels - a[p, g]) >= 10]
            a[p, g + 8] = far[np.random.randint(len(far))]
    return np.exp2(a.ravel()).repeat(32)


def f64(x):
    return np.asarray(x).astype(np.float64)


def striped8(idx):
    return np.asarray(idx).reshape(8, -1, 16).transpose(0, 2, 1).reshape(128, -1).astype(np.uint16)


def unstriped8(offs):
    return offs.reshape(8, 16, -1).transpose(0, 2, 1).reshape(8, -1).astype(np.int64)


def pick8(x, idx, run):
    r = np.arange(len(x))
    return x[r[:, None], idx[r % (8 * run) // run]]


E2M1 = np.array([0.0, 0.5, 1.0, 1.5, 2.0, 3.0, 4.0, 6.0, -0.0, -0.5, -1.0, -1.5, -2.0, -3.0, -4.0, -6.0])


def pack_weight(w, fmt):
    k, n = w.shape
    w = f64(np.asarray(w, np.float32).astype(ml_dtypes.bfloat16)).reshape(k // 32, 32, n)
    amax = np.abs(w).max(1)
    if fmt == "e4m3":
        byte = np.frexp(amax)[1] - 1 + 127 - 7
    else:
        mant, ex = np.frexp(amax / 6.0)
        byte = np.where(mant > 0.5, ex, ex - 1) + 127
    byte = np.clip(np.where(amax > 0, byte, 1), 1, 254)
    scaled = (w * np.exp2(127.0 - byte)[:, None, :]).reshape(k, n).astype(np.float32)
    by_word = np.ascontiguousarray(scaled.reshape(k // 512, 128, 4, n).transpose(0, 1, 3, 2))
    if fmt == "e4m3":
        words = by_word.astype(ml_dtypes.float8_e4m3fn).view(np.uint8)
    else:
        c = by_word.astype(ml_dtypes.float4_e2m1fn).view(np.uint8) & 0xF
        words = (c[..., 0::2] | (c[..., 1::2] << 4)).reshape(k // 512, 128, 2 * n)
    return np.ascontiguousarray(words), np.ascontiguousarray(byte.astype(np.uint8).reshape(k // 512, 16, n))


def unpack_weight(words, scales, fmt):
    g, _, n = scales.shape
    words = np.ascontiguousarray(words).reshape(g, 128, n, -1)
    if fmt == "e4m3":
        vals = words.view(ml_dtypes.float8_e4m3fn).astype(np.float64)
    else:
        nib = np.empty((g, 128, n, 4), np.uint8)
        nib[..., 0::2] = words & 0xF
        nib[..., 1::2] = words >> 4
        vals = E2M1[nib]
    vals = vals * np.repeat(np.exp2(scales.astype(np.float64) - 127.0), 8, axis=1)[..., None]
    return vals.transpose(0, 1, 3, 2).reshape(g * 512, n)


D, T, Z, I, Q, E = 512, 1024, 1024, 512, 512, 256


def setup_inputs():
    n = np.random.standard_normal
    idx = np.stack([np.random.permutation(T)[:I] for _ in range(8)])
    idx2 = np.stack([np.random.permutation(T)[:I] for _ in range(8)])
    idx3 = np.stack([np.random.permutation(T)[:I] for _ in range(8)])
    idx4 = np.stack([np.random.permutation(Z)[:I] for _ in range(8)])
    idx5 = np.stack([np.random.permutation(Z)[:I] for _ in range(8)])
    fd = mx_kscale(D)
    fq = mx_kscale(Q)
    cachep = pack_weight(n((D, T)) / fd[:, None], "e4m3")
    mixp = pack_weight(n((Q, E)) * 1.0 / np.sqrt(Q) / fq[:, None], "e2m1")
    return {
        "query": (n((D, Q)) * 1.0 / np.sqrt(D) * fd[:, None]).astype(np.float32),
        "cache_words": cachep[0],
        "cache_scales": cachep[1],
        "rowf": (np.random.uniform(0.5, 2.0, (Q, 1)) * fq[:, None]).astype(np.float32),
        "mix_words": mixp[0],
        "mix_scales": mixp[1],
        "offs": striped8(idx),
        "offs2": striped8(idx2),
        "offs3": striped8(idx3),
        "offs4": striped8(idx4),
        "offs5": striped8(idx5),
    }


def reference(query, cache_words, cache_scales, rowf, mix_words, mix_scales, offs, offs2, offs3, offs4, offs5):
    idx = unstriped8(offs)
    idx2 = unstriped8(offs2)
    idx3 = unstriped8(offs3)
    idx4 = unstriped8(offs4)
    idx5 = unstriped8(offs5)
    cacheu = unpack_weight(cache_words, cache_scales, "e4m3")
    mixu = unpack_weight(mix_words, mix_scales, "e2m1")
    queryq = mxq(f64(query), 0, "e4m3")
    a = queryq.T @ cacheu
    f1 = np.zeros((Q, T))
    f1[np.arange(Q)[:, None], idx2[np.arange(Q) % 512 // 64]] = pick8(a, idx, 64)
    c1 = a - f1
    g = pick8(c1, idx3, 64)
    gw = g * f64(rowf)
    gwq = mxq(gw, 0, "e4m3")
    o1 = mixu.T @ gwq
    pa = np.zeros((E, Z))
    pa[np.arange(E)[:, None], idx4[np.arange(E) % 128 // 16]] = o1
    pb = np.zeros((E, Z))
    pb[np.arange(E)[:, None], idx5[np.arange(E) % 128 // 16]] = o1
    y = pa - pb
    return y

@@ -1,0 +1,237 @@
+from contextlib import ExitStack
+
+import concourse.mybir as mybir
+
+D, T, Z, I, Q, E = 512, 1024, 1024, 512, 512, 256
+FLOPS = 2 * D * Q * T + 2 * Q * E * I
+
+F32 = mybir.dt.float32
+BF16 = mybir.dt.bfloat16
+I32 = mybir.dt.int32
+U32 = mybir.dt.uint32
+U16 = mybir.dt.uint16
+U8 = mybir.dt.uint8
+FP8X4 = mybir.dt.float8_e4m3fn_x4
+FP4X4 = mybir.dt.float4_e2m1fn_x4
+COPY = mybir.ActivationFunctionType.Copy
+SUB = mybir.AluOpType.subtract
+
+P = 128
+PACK = 4
+HALF = I // 2
+FIRST = 128
+M_VECTOR = 84
+QUARTER = T // 4
+
+
+def tile_attend_removed_one_twoposts_kernel(tc, query, cache_words, cache_scales, rowf, mix_words, mix_scales,
+                                             offs, offs2, offs3, offs4, offs5, out):
+    nc = tc.nc
+    with ExitStack() as ctx:
+        lists = ctx.enter_context(tc.tile_pool(name="lists", bufs=1))
+        keep = ctx.enter_context(tc.tile_pool(name="keep", bufs=1))
+        psum = ctx.enter_context(tc.psum_pool(name="psum", bufs=1))
+
+        def load_list(src, name):
+            t = lists.tile([P, I // 16], U16, name=name)
+            nc.sync.dma_start(t[:], src)
+            return t
+
+        def entries(lst, a, b):
+            return lst[:, a // 16 : b // 16]
+
+        cache_plane = keep.tile([P, QUARTER], U8, name="cache_plane", align_bytes=64)
+        nc.gpsimd.memset(cache_plane[:].bitcast(I32), 0)
+        mix_plane = keep.tile([P, E], U8, name="mix_plane", align_bytes=64)
+        nc.gpsimd.memset(mix_plane[:].bitcast(I32), 0)
+
+        q_raw = keep.tile([P, PACK, Q], F32, name="q_raw")
+        nc.sync.dma_start(q_raw[:], query.rearrange("(p j) q -> p j q", j=PACK))
+        for quad in range(4):
+            nc.sync.dma_start(
+                cache_plane[32 * quad : 32 * quad + 16, :].bitcast(I32),
+                cache_scales[0, 4 * quad : 4 * quad + 4, :].bitcast(I32).rearrange("r (u c) -> u r c", u=4),
+            )
+        cache_flat = cache_words[0].rearrange("p n t -> p (n t)")
+        cache_sb = keep.tile([P, T], I32, name="cache_sb", tag="cache_then_c1", align_bytes=64)
+        nc.sync.dma_start(cache_sb[:], cache_flat.bitcast(I32))
+        l1 = load_list(offs, "l1")
+        l2 = load_list(offs2, "l2")
+        l3 = load_list(offs3, "l3")
+        rf = keep.tile([P, PACK], F32, name="rf")
+        nc.sync.dma_start(rf[:], rowf.rearrange("(p t) o -> p (t o)", t=PACK))
+        mix_sb = keep.tile([P, 2 * E], U8, name="mix_sb", align_bytes=64)
+        nc.sync.dma_start(mix_sb[:].bitcast(I32), mix_words[0].bitcast(I32))
+        for quad in range(4):
+            nc.sync.dma_start(
+                mix_plane[32 * quad : 32 * quad + 4, :].bitcast(I32),
+                mix_scales[0, 4 * quad : 4 * quad + 4, :].bitcast(I32),
+            )
+        l4 = load_list(offs4, "l4")
+        l5 = load_list(offs5, "l5")
+
+        f1 = []
+        for b in range(2):
+            f = keep.tile([P, T], F32, name=f"f1_{b}")
+            nc.vector.memset(f[:].bitcast(I32), 0)
+            f1.append(f)
+
+        pages = []
+        for b in range(4):
+            pg = keep.tile([P, Z], F32, name=f"page{b}")
+            nc.vector.memset(pg[:].bitcast(I32), 0)
+            pages.append(pg)
+
+        q_bf = keep.tile([P, PACK * Q], BF16, name="q_bf", align_bytes=64)
+        q_dst = q_bf[:].rearrange("p (t m j) -> p m j t", t=PACK, j=PACK)
+        q_src = q_raw[:].rearrange("p j (m t) -> p m j t", t=PACK)
+        nc.vector.tensor_copy(q_dst[:, :M_VECTOR], q_src[:, :M_VECTOR])
+        nc.scalar.activation(q_dst[:, M_VECTOR:], q_src[:, M_VECTOR:], COPY)
+        q_codes = keep.tile([P, Q], U32, name="q_codes", tag="codes_then_c1", align_bytes=64)
+        q_plane = keep.tile([P, Q], U8, name="q_plane", align_bytes=64)
+        nc.vector.quantize_mx(q_codes[:, :P].bitcast(FP8X4), q_plane[:, :P], q_bf[:, : PACK * P])
+        nc.vector.quantize_mx(q_codes[:, P:].bitcast(FP8X4), q_plane[:, P:], q_bf[:, PACK * P :])
+
+        a = [keep.tile([P, T], F32, name=f"a{t}") for t in range(PACK)]
+        picked = [keep.tile([P, I], F32, name=f"picked{t}") for t in range(PACK)]
+        c1 = {}
+        c1_tags = ("cache_then_c1", "codes_then_c1", "c1_2", "c1_3")
+        g = keep.tile([P, PACK, I], F32, name="g")
+
+        def score(dst, t, u):
+            nc.tensor.matmul_mx(
+                dst,
+                lhsT=q_codes[:, t * P : (t + 1) * P].bitcast(FP8X4),
+                lhsT_scale=q_plane[:, t * P : (t + 1) * P],
+                rhs=cache_sb[:, u * QUARTER : (u + 1) * QUARTER].bitcast(FP8X4),
+                rhs_scale=cache_plane[4 * u :, :],
+                start=True,
+                stop=True,
+            )
+
+        def bank(b, width):
+            return psum.tile([P, width], F32, name=f"bank{b}", tag=f"bank{b}")
+
+        def score_half(t, h, b):
+            acc = bank(b, 2 * QUARTER)
+            for v in range(2):
+                score(acc[:, v * QUARTER : (v + 1) * QUARTER], t, 2 * h + v)
+            return acc
+
+        def pick(t, lo, hi):
+            nc.vector.tensor_copy(picked[t][:, lo:hi], a[t][:].indirect(entries(l1, lo, hi)))
+
+        def place(t, lo, hi):
+            nc.scalar.activation(f1[t % 2][:].indirect(entries(l2, lo, hi)), picked[t][:, lo:hi], COPY)
+
+        def remove(t):
+            c1[t] = keep.tile([P, T], F32, name=f"c1_{t}", tag=c1_tags[t], align_bytes=64)
+            nc.vector.tensor_tensor(c1[t][:], a[t][:], f1[t % 2][:], SUB)
+
+        def look_vector(t, lo, hi):
+            nc.vector.tensor_copy(g[:, t, lo:hi], c1[t][:].indirect(entries(l3, lo, hi)))
+
+        def weigh(t, lo, hi):
+            nc.vector.tensor_scalar_mul(g[:, t, lo:hi], g[:, t, lo:hi], rf[:, t : t + 1])
+
+        def look_scalar(t, lo, hi):
+            nc.scalar.activation(g[:, t, lo:hi], c1[t][:].indirect(entries(l3, lo, hi)), COPY, scale=rf[:, t : t + 1])
+
+        for u in range(4):
+            acc = bank(u, QUARTER)
+            score(acc[:], 0, u)
+            dst = a[0][:, u * QUARTER : (u + 1) * QUARTER]
+            if u % 2 == 0:
+                nc.vector.tensor_copy(dst, acc[:])
+            else:
+                nc.scalar.activation(dst, acc[:], COPY)
+        accs = {}
+        for t, b0 in ((1, 4), (2, 6), (3, 0)):
+            for h in range(2):
+                accs[t, h] = score_half(t, h, b0 + h)
+
+        def empty_vector(t, h):
+            nc.vector.tensor_copy(a[t][:, h * (T // 2) : (h + 1) * (T // 2)], accs[t, h][:])
+
+        pick(0, 0, HALF)
+        nc.scalar.activation(a[1][:, : T // 2], accs[1, 0][:], COPY)
+        place(0, 0, HALF)
+        pick(0, HALF, I)
+        place(0, HALF, I)
+        empty_vector(1, 1)
+        pick(1, 0, I)
+        place(1, 0, I)
+        empty_vector(2, 0)
+        empty_vector(2, 1)
+        remove(0)
+        pick(2, 0, I)
+        place(2, 0, I)
+        empty_vector(3, 0)
+        empty_vector(3, 1)
+        remove(1)
+        pick(3, 0, I)
+        place(3, 0, I)
+        look_vector(0, 0, I)
+        remove(2)
+        look_vector(1, 0, I)
+        look_vector(2, HALF, I)
+        weigh(0, 0, I)
+        look_scalar(2, 0, HALF)
+        remove(3)
+        weigh(1, 0, I)
+        weigh(2, HALF, I)
+        look_scalar(3, 0, HALF)
+        look_scalar(3, HALF, I)
+
+
+        o1 = [keep.tile([P, I], F32, name=f"o1_{h}") for h in range(2)]
+
+        def quantise(lo, hi, name):
+            n = hi - lo
+            gw = keep.tile([P, PACK * n], BF16, name=f"gw_{name}", tag="gw", align_bytes=64)
+            nc.vector.tensor_copy(
+                gw[:].rearrange("p (c i t) -> p c t i", i=4, t=PACK),
+                g[:, :, lo:hi].rearrange("p t (c i) -> p c t i", i=4),
+            )
+            codes = keep.tile([P, n], U32, name=f"gw_codes_{name}", align_bytes=64)
+            plane = keep.tile([P, n], U8, name=f"gw_plane_{name}", align_bytes=64)
+            nc.vector.quantize_mx(codes[:].bitcast(FP8X4), plane[:], gw[:])
+            return codes, plane
+
+        def mix(codes, plane, lo, hi, h, b):
+            acc = bank(b, hi - lo)
+            nc.tensor.matmul_mx(
+                acc[:],
+                lhsT=mix_sb[:, 2 * P * h : 2 * P * (h + 1)].bitcast(FP4X4),
+                lhsT_scale=mix_plane[:, P * h : P * (h + 1)],
+                rhs=codes[:, lo:hi].bitcast(FP8X4),
+                rhs_scale=plane[:, lo:hi],
+                start=True,
+                stop=True,
+            )
+            return acc
+
+        def post(h, lo, hi):
+            for lst, pg in ((l4, pages[2 * h]), (l5, pages[2 * h + 1])):
+                nc.scalar.activation(pg[:].indirect(entries(lst, lo, hi)), o1[h][:, lo:hi], COPY)
+
+        codes, plane = quantise(0, FIRST, "first")
+        for h in range(2):
+            acc = mix(codes, plane, 0, FIRST, h, 2 + h)
+            nc.scalar.activation(o1[h][:, :FIRST], acc[:], COPY)
+        for h in range(2):
+            post(h, 0, FIRST)
+        codes, plane = quantise(FIRST, I, "rest")
+        for h in range(2):
+            for k, (lo, hi) in enumerate(((0, FIRST), (FIRST, I - FIRST))):
+                acc = mix(codes, plane, lo, hi, h, 4 + 2 * h + k)
+                nc.vector.tensor_copy(o1[h][:, FIRST + lo : FIRST + hi], acc[:])
+        for h in range(2):
+            post(h, FIRST, I)
+            res = keep.tile([P, Z], F32, name=f"res{h}")
+            pieces = 1 if h == 0 else 4
+            w = Z // pieces
+            for k in range(pieces):
+                cols = slice(k * w, (k + 1) * w)
+                nc.vector.tensor_tensor(res[:, cols], pages[2 * h][:, cols], pages[2 * h + 1][:, cols], SUB)
+                nc.sync.dma_start(out[h * P : (h + 1) * P, cols], res[:, cols])

@@ -45,8 +45,12 @@ def tile_attend_removed_one_twoposts_kernel(tc, query, cache_words, cache_scales
         mix_plane = keep.tile([P, E], U8, name="mix_plane", align_bytes=64)
         nc.gpsimd.memset(mix_plane[:].bitcast(I32), 0)
 
-        q_raw = keep.tile([P, PACK, Q], F32, name="q_raw")
-        nc.sync.dma_start(q_raw[:], query.rearrange("(p j) q -> p j q", j=PACK))
+        q_rows = query.rearrange("(p j) q -> p j q", j=PACK)
+        q_raw = []
+        for pair in range(2):
+            r = keep.tile([P, 2, Q], F32, name=f"q_raw{pair}")
+            nc.sync.dma_start(r[:], q_rows[:, 2 * pair : 2 * pair + 2, :])
+            q_raw.append(r)
         for quad in range(4):
             nc.sync.dma_start(
                 cache_plane[32 * quad : 32 * quad + 16, :].bitcast(I32),
@@ -76,24 +80,23 @@ def tile_attend_removed_one_twoposts_kernel(tc, query, cache_words, cache_scales
             nc.vector.memset(f[:].bitcast(I32), 0)
             f1.append(f)
 
-        pages = []
-        for b in range(4):
-            pg = keep.tile([P, Z], F32, name=f"page{b}")
-            nc.vector.memset(pg[:].bitcast(I32), 0)
-            pages.append(pg)
+        pages = [keep.tile([P, Z], F32, name="page0")]
+        nc.vector.memset(pages[0][:].bitcast(I32), 0)
 
         q_bf = keep.tile([P, PACK * Q], BF16, name="q_bf", align_bytes=64)
         q_dst = q_bf[:].rearrange("p (t m j) -> p m j t", t=PACK, j=PACK)
-        q_src = q_raw[:].rearrange("p j (m t) -> p m j t", t=PACK)
-        nc.vector.tensor_copy(q_dst[:, :M_VECTOR], q_src[:, :M_VECTOR])
-        nc.scalar.activation(q_dst[:, M_VECTOR:], q_src[:, M_VECTOR:], COPY)
+        for pair in range(2):
+            q_src = q_raw[pair][:].rearrange("p j (m t) -> p m j t", t=PACK)
+            rows = slice(2 * pair, 2 * pair + 2)
+            nc.vector.tensor_copy(q_dst[:, :M_VECTOR, rows], q_src[:, :M_VECTOR])
+            nc.scalar.activation(q_dst[:, M_VECTOR:, rows], q_src[:, M_VECTOR:], COPY)
         q_codes = keep.tile([P, Q], U32, name="q_codes", tag="codes_then_c1", align_bytes=64)
         q_plane = keep.tile([P, Q], U8, name="q_plane", align_bytes=64)
         nc.vector.quantize_mx(q_codes[:, :P].bitcast(FP8X4), q_plane[:, :P], q_bf[:, : PACK * P])
         nc.vector.quantize_mx(q_codes[:, P:].bitcast(FP8X4), q_plane[:, P:], q_bf[:, PACK * P :])
 
         a = [keep.tile([P, T], F32, name=f"a{t}") for t in range(PACK)]
-        picked = [keep.tile([P, I], F32, name=f"picked{t}") for t in range(PACK)]
+        picked = [keep.tile([P, I], F32, name=f"picked{t}", tag=f"picked_then_page{t}") for t in range(PACK)]
         c1 = {}
         c1_tags = ("cache_then_c1", "codes_then_c1", "c1_2", "c1_3")
         g = keep.tile([P, PACK, I], F32, name="g")
@@ -124,6 +127,11 @@ def tile_attend_removed_one_twoposts_kernel(tc, query, cache_words, cache_scales
         def place(t, lo, hi):
             nc.scalar.activation(f1[t % 2][:].indirect(entries(l2, lo, hi)), picked[t][:, lo:hi], COPY)
 
+        def clear_page(t):
+            pg = keep.tile([P, Z], F32, name=f"page{t + 1}", tag=f"picked_then_page{t}")
+            nc.gpsimd.memset(pg[:].bitcast(I32), 0)
+            pages.append(pg)
+
         def remove(t):
             c1[t] = keep.tile([P, T], F32, name=f"c1_{t}", tag=c1_tags[t], align_bytes=64)
             nc.vector.tensor_tensor(c1[t][:], a[t][:], f1[t % 2][:], SUB)
@@ -145,60 +153,62 @@ def tile_attend_removed_one_twoposts_kernel(tc, query, cache_words, cache_scales
                 nc.vector.tensor_copy(dst, acc[:])
             else:
                 nc.scalar.activation(dst, acc[:], COPY)
+        for u in range(2):
+            acc = bank(4 + u, QUARTER)
+            score(acc[:], 1, u)
+            nc.scalar.activation(a[1][:, u * QUARTER : (u + 1) * QUARTER], acc[:], COPY)
         accs = {}
-        for t, b0 in ((1, 4), (2, 6), (3, 0)):
-            for h in range(2):
-                accs[t, h] = score_half(t, h, b0 + h)
+        for k, (t, h) in enumerate(((1, 1), (2, 0), (2, 1), (3, 0), (3, 1))):
+            accs[t, h] = score_half(t, h, (6 + k) % 8)
 
         def empty_vector(t, h):
             nc.vector.tensor_copy(a[t][:, h * (T // 2) : (h + 1) * (T // 2)], accs[t, h][:])
 
         pick(0, 0, HALF)
-        nc.scalar.activation(a[1][:, : T // 2], accs[1, 0][:], COPY)
         place(0, 0, HALF)
+        empty_vector(1, 1)
         pick(0, HALF, I)
         place(0, HALF, I)
-        empty_vector(1, 1)
         pick(1, 0, I)
         place(1, 0, I)
         empty_vector(2, 0)
         empty_vector(2, 1)
         remove(0)
+        clear_page(0)
         pick(2, 0, I)
         place(2, 0, I)
         empty_vector(3, 0)
         empty_vector(3, 1)
         remove(1)
+        clear_page(1)
         pick(3, 0, I)
         place(3, 0, I)
         look_vector(0, 0, I)
         remove(2)
+        clear_page(2)
         look_vector(1, 0, I)
-        look_vector(2, HALF, I)
-        weigh(0, 0, I)
         look_scalar(2, 0, HALF)
         remove(3)
+        weigh(0, 0, I)
         weigh(1, 0, I)
-        weigh(2, HALF, I)
         look_scalar(3, 0, HALF)
         look_scalar(3, HALF, I)
 
 
         o1 = [keep.tile([P, I], F32, name=f"o1_{h}") for h in range(2)]
 
-        def quantise(lo, hi, name):
-            n = hi - lo
-            gw = keep.tile([P, PACK * n], BF16, name=f"gw_{name}", tag="gw", align_bytes=64)
+        codes = keep.tile([P, I], U32, name="gw_codes", align_bytes=64)
+        plane = keep.tile([P, I], U8, name="gw_plane", align_bytes=64)
+
+        def quantise(lo, hi):
+            gw = keep.tile([P, PACK * (hi - lo)], BF16, name=f"gw_{lo}", tag="gw", align_bytes=64)
             nc.vector.tensor_copy(
                 gw[:].rearrange("p (c i t) -> p c t i", i=4, t=PACK),
                 g[:, :, lo:hi].rearrange("p t (c i) -> p c t i", i=4),
             )
-            codes = keep.tile([P, n], U32, name=f"gw_codes_{name}", align_bytes=64)
-            plane = keep.tile([P, n], U8, name=f"gw_plane_{name}", align_bytes=64)
-            nc.vector.quantize_mx(codes[:].bitcast(FP8X4), plane[:], gw[:])
-            return codes, plane
+            nc.vector.quantize_mx(codes[:, lo:hi].bitcast(FP8X4), plane[:, lo:hi], gw[:])
 
-        def mix(codes, plane, lo, hi, h, b):
+        def mix(lo, hi, h, b):
             acc = bank(b, hi - lo)
             nc.tensor.matmul_mx(
                 acc[:],
@@ -215,23 +225,23 @@ def tile_attend_removed_one_twoposts_kernel(tc, query, cache_words, cache_scales
             for lst, pg in ((l4, pages[2 * h]), (l5, pages[2 * h + 1])):
                 nc.scalar.activation(pg[:].indirect(entries(lst, lo, hi)), o1[h][:, lo:hi], COPY)
 
-        codes, plane = quantise(0, FIRST, "first")
+        quantise(0, FIRST)
+        nc.scalar.activation(o1[0][:, :FIRST], mix(0, FIRST, 0, 3)[:], COPY)
+        post(0, 0, FIRST)
+        quantise(FIRST, HALF)
+        nc.vector.tensor_copy(o1[1][:, :HALF], mix(0, HALF, 1, 4)[:])
+        post(1, 0, HALF)
+        look_vector(2, HALF, I)
+        nc.vector.tensor_copy(o1[0][:, FIRST:HALF], mix(FIRST, HALF, 0, 5)[:])
+        weigh(2, HALF, I)
+        quantise(HALF, I)
         for h in range(2):
-            acc = mix(codes, plane, 0, FIRST, h, 2 + h)
-            nc.scalar.activation(o1[h][:, :FIRST], acc[:], COPY)
-        for h in range(2):
-            post(h, 0, FIRST)
-        codes, plane = quantise(FIRST, I, "rest")
-        for h in range(2):
-            for k, (lo, hi) in enumerate(((0, FIRST), (FIRST, I - FIRST))):
-                acc = mix(codes, plane, lo, hi, h, 4 + 2 * h + k)
-                nc.vector.tensor_copy(o1[h][:, FIRST + lo : FIRST + hi], acc[:])
-        for h in range(2):
-            post(h, FIRST, I)
+            nc.vector.tensor_copy(o1[h][:, HALF:], mix(HALF, I, h, 6 + h)[:])
+        for h, lo in ((0, FIRST), (1, HALF)):
+            post(h, lo, I)
             res = keep.tile([P, Z], F32, name=f"res{h}")
-            pieces = 1 if h == 0 else 4
-            w = Z // pieces
-            for k in range(pieces):
-                cols = slice(k * w, (k + 1) * w)
+            cuts = (0, Z) if h == 0 else (0, Z // 2, Z - Z // 8, Z)
+            for k in range(len(cuts) - 1):
+                cols = slice(cuts[k], cuts[k + 1])
                 nc.vector.tensor_tensor(res[:, cols], pages[2 * h][:, cols], pages[2 * h + 1][:, cols], SUB)
                 nc.sync.dma_start(out[h * P : (h + 1) * P, cols], res[:, cols])

from contextlib import ExitStack

import concourse.mybir as mybir

D, T, Z, I, Q, E = 512, 1024, 1024, 512, 512, 256
FLOPS = 2 * D * Q * T + 2 * Q * E * I

F32 = mybir.dt.float32
BF16 = mybir.dt.bfloat16
I32 = mybir.dt.int32
U32 = mybir.dt.uint32
U16 = mybir.dt.uint16
U8 = mybir.dt.uint8
FP8X4 = mybir.dt.float8_e4m3fn_x4
FP4X4 = mybir.dt.float4_e2m1fn_x4
COPY = mybir.ActivationFunctionType.Copy
SUB = mybir.AluOpType.subtract

P = 128
PACK = 4
HALF = I // 2
FIRST = 128
M_VECTOR = 84
QUARTER = T // 4


def tile_attend_removed_one_twoposts_kernel(tc, query, cache_words, cache_scales, rowf, mix_words, mix_scales,
                                             offs, offs2, offs3, offs4, offs5, out):
    nc = tc.nc
    with ExitStack() as ctx:
        lists = ctx.enter_context(tc.tile_pool(name="lists", bufs=1))
        keep = ctx.enter_context(tc.tile_pool(name="keep", bufs=1))
        psum = ctx.enter_context(tc.psum_pool(name="psum", bufs=1))

        def load_list(src, name):
            t = lists.tile([P, I // 16], U16, name=name)
            nc.sync.dma_start(t[:], src)
            return t

        def entries(lst, a, b):
            return lst[:, a // 16 : b // 16]

        cache_plane = keep.tile([P, QUARTER], U8, name="cache_plane", align_bytes=64)
        nc.gpsimd.memset(cache_plane[:].bitcast(I32), 0)
        mix_plane = keep.tile([P, E], U8, name="mix_plane", align_bytes=64)
        nc.gpsimd.memset(mix_plane[:].bitcast(I32), 0)

        q_rows = query.rearrange("(p j) q -> p j q", j=PACK)
        q_raw = []
        for pair in range(2):
            r = keep.tile([P, 2, Q], F32, name=f"q_raw{pair}")
            nc.sync.dma_start(r[:], q_rows[:, 2 * pair : 2 * pair + 2, :])
            q_raw.append(r)
        for quad in range(4):
            nc.sync.dma_start(
                cache_plane[32 * quad : 32 * quad + 16, :].bitcast(I32),
                cache_scales[0, 4 * quad : 4 * quad + 4, :].bitcast(I32).rearrange("r (u c) -> u r c", u=4),
            )
        cache_flat = cache_words[0].rearrange("p n t -> p (n t)")
        cache_sb = keep.tile([P, T], I32, name="cache_sb", tag="cache_then_c1", align_bytes=64)
        nc.sync.dma_start(cache_sb[:], cache_flat.bitcast(I32))
        l1 = load_list(offs, "l1")
        l2 = load_list(offs2, "l2")
        l3 = load_list(offs3, "l3")
        rf = keep.tile([P, PACK], F32, name="rf")
        nc.sync.dma_start(rf[:], rowf.rearrange("(p t) o -> p (t o)", t=PACK))
        mix_sb = keep.tile([P, 2 * E], U8, name="mix_sb", align_bytes=64)
        nc.sync.dma_start(mix_sb[:].bitcast(I32), mix_words[0].bitcast(I32))
        for quad in range(4):
            nc.sync.dma_start(
                mix_plane[32 * quad : 32 * quad + 4, :].bitcast(I32),
                mix_scales[0, 4 * quad : 4 * quad + 4, :].bitcast(I32),
            )
        l4 = load_list(offs4, "l4")
        l5 = load_list(offs5, "l5")

        f1 = []
        for b in range(2):
            f = keep.tile([P, T], F32, name=f"f1_{b}")
            nc.vector.memset(f[:].bitcast(I32), 0)
            f1.append(f)

        pages = [keep.tile([P, Z], F32, name="page0")]
        nc.vector.memset(pages[0][:].bitcast(I32), 0)

        q_bf = keep.tile([P, PACK * Q], BF16, name="q_bf", align_bytes=64)
        q_dst = q_bf[:].rearrange("p (t m j) -> p m j t", t=PACK, j=PACK)
        for pair in range(2):
            q_src = q_raw[pair][:].rearrange("p j (m t) -> p m j t", t=PACK)
            rows = slice(2 * pair, 2 * pair + 2)
            nc.vector.tensor_copy(q_dst[:, :M_VECTOR, rows], q_src[:, :M_VECTOR])
            nc.scalar.activation(q_dst[:, M_VECTOR:, rows], q_src[:, M_VECTOR:], COPY)
        q_codes = keep.tile([P, Q], U32, name="q_codes", tag="codes_then_c1", align_bytes=64)
        q_plane = keep.tile([P, Q], U8, name="q_plane", align_bytes=64)
        nc.vector.quantize_mx(q_codes[:, :P].bitcast(FP8X4), q_plane[:, :P], q_bf[:, : PACK * P])
        nc.vector.quantize_mx(q_codes[:, P:].bitcast(FP8X4), q_plane[:, P:], q_bf[:, PACK * P :])

        a = [keep.tile([P, T], F32, name=f"a{t}") for t in range(PACK)]
        picked = [keep.tile([P, I], F32, name=f"picked{t}", tag=f"picked_then_page{t}") for t in range(PACK)]
        c1 = {}
        c1_tags = ("cache_then_c1", "codes_then_c1", "c1_2", "c1_3")
        g = keep.tile([P, PACK, I], F32, name="g")

        def score(dst, t, u):
            nc.tensor.matmul_mx(
                dst,
                lhsT=q_codes[:, t * P : (t + 1) * P].bitcast(FP8X4),
                lhsT_scale=q_plane[:, t * P : (t + 1) * P],
                rhs=cache_sb[:, u * QUARTER : (u + 1) * QUARTER].bitcast(FP8X4),
                rhs_scale=cache_plane[4 * u :, :],
                start=True,
                stop=True,
            )

        def bank(b, width):
            return psum.tile([P, width], F32, name=f"bank{b}", tag=f"bank{b}")

        def score_half(t, h, b):
            acc = bank(b, 2 * QUARTER)
            for v in range(2):
                score(acc[:, v * QUARTER : (v + 1) * QUARTER], t, 2 * h + v)
            return acc

        def pick(t, lo, hi):
            nc.vector.tensor_copy(picked[t][:, lo:hi], a[t][:].indirect(entries(l1, lo, hi)))

        def place(t, lo, hi):
            nc.scalar.activation(f1[t % 2][:].indirect(entries(l2, lo, hi)), picked[t][:, lo:hi], COPY)

        def clear_page(t):
            pg = keep.tile([P, Z], F32, name=f"page{t + 1}", tag=f"picked_then_page{t}")
            nc.gpsimd.memset(pg[:].bitcast(I32), 0)
            pages.append(pg)

        def remove(t):
            c1[t] = keep.tile([P, T], F32, name=f"c1_{t}", tag=c1_tags[t], align_bytes=64)
            nc.vector.tensor_tensor(c1[t][:], a[t][:], f1[t % 2][:], SUB)

        def look_vector(t, lo, hi):
            nc.vector.tensor_copy(g[:, t, lo:hi], c1[t][:].indirect(entries(l3, lo, hi)))

        def weigh(t, lo, hi):
            nc.vector.tensor_scalar_mul(g[:, t, lo:hi], g[:, t, lo:hi], rf[:, t : t + 1])

        def look_scalar(t, lo, hi):
            nc.scalar.activation(g[:, t, lo:hi], c1[t][:].indirect(entries(l3, lo, hi)), COPY, scale=rf[:, t : t + 1])

        for u in range(4):
            acc = bank(u, QUARTER)
            score(acc[:], 0, u)
            dst = a[0][:, u * QUARTER : (u + 1) * QUARTER]
            if u % 2 == 0:
                nc.vector.tensor_copy(dst, acc[:])
            else:
                nc.scalar.activation(dst, acc[:], COPY)
        for u in range(2):
            acc = bank(4 + u, QUARTER)
            score(acc[:], 1, u)
            nc.scalar.activation(a[1][:, u * QUARTER : (u + 1) * QUARTER], acc[:], COPY)
        accs = {}
        for k, (t, h) in enumerate(((1, 1), (2, 0), (2, 1), (3, 0), (3, 1))):
            accs[t, h] = score_half(t, h, (6 + k) % 8)

        def empty_vector(t, h):
            nc.vector.tensor_copy(a[t][:, h * (T // 2) : (h + 1) * (T // 2)], accs[t, h][:])

        pick(0, 0, HALF)
        place(0, 0, HALF)
        empty_vector(1, 1)
        pick(0, HALF, I)
        place(0, HALF, I)
        pick(1, 0, I)
        place(1, 0, I)
        empty_vector(2, 0)
        empty_vector(2, 1)
        remove(0)
        clear_page(0)
        pick(2, 0, I)
        place(2, 0, I)
        empty_vector(3, 0)
        empty_vector(3, 1)
        remove(1)
        clear_page(1)
        pick(3, 0, I)
        place(3, 0, I)
        look_vector(0, 0, I)
        remove(2)
        clear_page(2)
        look_vector(1, 0, I)
        look_scalar(2, 0, HALF)
        remove(3)
        weigh(0, 0, I)
        weigh(1, 0, I)
        look_scalar(3, 0, HALF)
        look_scalar(3, HALF, I)


        o1 = [keep.tile([P, I], F32, name=f"o1_{h}") for h in range(2)]

        codes = keep.tile([P, I], U32, name="gw_codes", align_bytes=64)
        plane = keep.tile([P, I], U8, name="gw_plane", align_bytes=64)

        def quantise(lo, hi):
            gw = keep.tile([P, PACK * (hi - lo)], BF16, name=f"gw_{lo}", tag="gw", align_bytes=64)
            nc.vector.tensor_copy(
                gw[:].rearrange("p (c i t) -> p c t i", i=4, t=PACK),
                g[:, :, lo:hi].rearrange("p t (c i) -> p c t i", i=4),
            )
            nc.vector.quantize_mx(codes[:, lo:hi].bitcast(FP8X4), plane[:, lo:hi], gw[:])

        def mix(lo, hi, h, b):
            acc = bank(b, hi - lo)
            nc.tensor.matmul_mx(
                acc[:],
                lhsT=mix_sb[:, 2 * P * h : 2 * P * (h + 1)].bitcast(FP4X4),
                lhsT_scale=mix_plane[:, P * h : P * (h + 1)],
                rhs=codes[:, lo:hi].bitcast(FP8X4),
                rhs_scale=plane[:, lo:hi],
                start=True,
                stop=True,
            )
            return acc

        def post(h, lo, hi):
            for lst, pg in ((l4, pages[2 * h]), (l5, pages[2 * h + 1])):
                nc.scalar.activation(pg[:].indirect(entries(lst, lo, hi)), o1[h][:, lo:hi], COPY)

        quantise(0, FIRST)
        nc.scalar.activation(o1[0][:, :FIRST], mix(0, FIRST, 0, 3)[:], COPY)
        post(0, 0, FIRST)
        quantise(FIRST, HALF)
        nc.vector.tensor_copy(o1[1][:, :HALF], mix(0, HALF, 1, 4)[:])
        post(1, 0, HALF)
        look_vector(2, HALF, I)
        nc.vector.tensor_copy(o1[0][:, FIRST:HALF], mix(FIRST, HALF, 0, 5)[:])
        weigh(2, HALF, I)
        quantise(HALF, I)
        for h in range(2):
            nc.vector.tensor_copy(o1[h][:, HALF:], mix(HALF, I, h, 6 + h)[:])
        for h, lo in ((0, FIRST), (1, HALF)):
            post(h, lo, I)
            res = keep.tile([P, Z], F32, name=f"res{h}")
            cuts = (0, Z) if h == 0 else (0, Z // 2, Z - Z // 8, Z)
            for k in range(len(cuts) - 1):
                cols = slice(cuts[k], cuts[k + 1])
                nc.vector.tensor_tensor(res[:, cols], pages[2 * h][:, cols], pages[2 * h + 1][:, cols], SUB)
                nc.sync.dma_start(out[h * P : (h + 1) * P, cols], res[:, cols])
